import numpy as np
import ml_dtypes


def mxq(x, axis, fmt="e4m3"):
    dtype, down = {"e4m3": (ml_dtypes.float8_e4m3fn, 7), "e5m2": (ml_dtypes.float8_e5m2, 14)}[fmt]
    v = np.moveaxis(np.asarray(x, np.float32).astype(ml_dtypes.bfloat16).astype(np.float64), axis, -1)
    blocks = v.reshape(v.shape[:-1] + (-1, 32))
    amax = np.abs(blocks).max(-1, keepdims=True)
    byte = np.maximum(np.where(amax > 0, np.frexp(amax)[1] - 1 + 127, 0) - down, 1)
    scale = np.exp2(byte - 127.0)
    codes = (blocks / scale).astype(np.float32).astype(dtype).astype(np.float64)
    return np.moveaxis((codes * scale).reshape(v.shape), -1, axis)


WIDE = False


def mx_kscale(k):
    if not WIDE:
        return np.ones(k)
    levels = np.array([10, -10, 5, -5, 0])
    if k % 512:
        return np.exp2(np.random.permutation(np.resize(levels, k // 32))).repeat(32)
    a = np.empty((k // 512, 16))
    for p in range(k // 512):
        a[p, :8] = np.random.permutation(np.resize(levels, 8))
        for g in range(8):
            far = levels[np.abs(levels - a[p, g]) >= 10]
            a[p, g + 8] = far[np.random.randint(len(far))]
    return np.exp2(a.ravel()).repeat(32)


def f64(x):
    return np.asarray(x).astype(np.float64)


def striped(idx):
    return np.tile(idx.reshape(-1, 16).T, (8, 1)).astype(np.uint16)


def unstriped(offs):
    return offs[:16].T.reshape(-1).astype(np.int64)


K, T, E, C, N = 512, 512, 16, 128, 256
TOP = 4


def by_expert(wq, xq):
    return np.concatenate([wq[e].T @ xq[:, e * C:(e + 1) * C] for e in range(E)], axis=1)


def setup_inputs():
    n = np.random.standard_normal
    s = mx_kscale(K)[:, None]
    deal = np.repeat(np.arange(E), C).reshape(TOP, T)[:, np.random.permutation(T)]
    deal = np.take_along_axis(deal, np.argsort(np.random.rand(TOP, T), axis=0), axis=0)
    for _ in range(8):
        s_, t_ = np.random.permutation(T).reshape(2, -1); r = np.random.randint(TOP, size=T // 2); x, y = deal[r, s_].copy(), deal[r, t_].copy()
        ok = ~((deal[:, s_] == y).any(0) | (deal[:, t_] == x).any(0)); deal[r[ok], s_[ok]] = y[ok]; deal[r[ok], t_[ok]] = x[ok]
    order = np.lexsort((np.random.rand(TOP * T), deal.reshape(-1)))
    slot_token = order % T; pos = np.empty(TOP * T, np.int64); pos[order] = np.arange(TOP * T); pos = pos.reshape(TOP, T)
    g = np.random.uniform(0.5, 1.5, (TOP, T)); g = g / g.sum(0)
    return {
        "xT": (n((K, T)) * s).astype(np.float32),
        "w": (n((E + 1, K, N)) / np.sqrt(K) / s[None]).astype(np.float32),
        "b": (0.3 * n((N, E + 1))).astype(np.float32),
        "gate": np.stack([np.tile(r, (N, 1)) for r in g]).astype(np.float32),
        "offs": striped(slot_token),
        "pos1": striped(pos[0]),
        "pos2": striped(pos[1]),
        "pos3": striped(pos[2]),
        "pos4": striped(pos[3]),
    }


def reference(xT, w, b, gate, offs, pos1, pos2, pos3, pos4):
    idx = unstriped(offs)
    wq = mxq(f64(w), 1, "e4m3")
    xs = mxq(f64(xT), 0, "e4m3")
    ys = (wq[E].T @ xs) + f64(b)[:, E:]
    xq = mxq(f64(xT)[:, idx], 0, "e4m3")
    y = by_expert(wq, xq)
    y = y + np.repeat(f64(b)[:, :E], C, axis=1)
    return ys + sum(f64(gate[r]) * y[:, unstriped(p)] for r, p in enumerate((pos1, pos2, pos3, pos4)))

@@ -1,0 +1,286 @@
+from contextlib import ExitStack
+
+import concourse.mybir as mybir
+from concourse.masks import make_identity
+
+K, T, E, C, N, TOP = 512, 512, 16, 128, 256, 4
+S = E * C
+FLOPS = 2 * K * N * (S + T)
+
+F32 = mybir.dt.float32
+BF16 = mybir.dt.bfloat16
+I32 = mybir.dt.int32
+U32 = mybir.dt.uint32
+U16 = mybir.dt.uint16
+U8 = mybir.dt.uint8
+FP8X4 = mybir.dt.float8_e4m3fn_x4
+ADD = mybir.AluOpType.add
+MULT = mybir.AluOpType.mult
+IDENT = mybir.ActivationFunctionType.Identity
+
+P = 128
+PACK = 4
+HALVES = N // P
+GROUP = 4
+GROUPS = E // GROUP
+GS = GROUP * C
+WIN = 704
+WCOLS = N * PACK
+UNIT = 256
+BLOCKS = UNIT // P
+TURNED = TOP - 1
+
+
+def tile_moe_shr_lin_bias_kernel(tc, xT, w, b, gate, offs, pos1, pos2, pos3, pos4, out):
+    nc = tc.nc
+    with ExitStack() as ctx:
+        keep = ctx.enter_context(tc.tile_pool(name="keep", bufs=1))
+        wraw = ctx.enter_context(tc.tile_pool(name="wraw", bufs=12))
+        psum_a = ctx.enter_context(tc.psum_pool(name="psum_a", bufs=4))
+        psum_b = ctx.enter_context(tc.psum_pool(name="psum_b", bufs=4))
+
+        x_rows = xT.rearrange("(p j) t -> p j t", j=PACK)
+        x_raw = [keep.tile([P, 2, T], F32, name=f"x_raw{u}") for u in range(2)]
+        offs_t = keep.tile([P, S // 16], U16, name="offs_t")
+        pos_t = [keep.tile([P, T // 16], U16, name=f"pos_t{r}") for r in range(TOP)]
+        bias = keep.tile([P, HALVES, 32], F32, name="bias")
+        gate_rows = keep.tile([P, T], F32, name="gate_rows")
+        gate_last = keep.tile([P, T], F32, name="gate_last")
+        gate_cols = keep.tile([P, T // P, TOP], F32, name="gate_cols")
+        ident = keep.tile([P, P], F32, name="ident")
+        pairs = keep.tile([P, 2 * WIN * 2], BF16, name="pairs", align_bytes=64)
+        y = [keep.tile([P, S], F32, name=f"y{h}") for h in range(HALVES)]
+        w_bf = [keep.tile([P, GROUP * WCOLS], BF16, name=f"w_bf{g}", align_bytes=64) for g in range(GROUPS - 1)]
+        w_bf_late = keep.tile([P, 2 * WCOLS], BF16, name="w_bf_late", align_bytes=64)
+        w_bf_shared = keep.tile([P, WCOLS], BF16, name="w_bf_shared", align_bytes=64)
+        w_place = [(w_bf[e // GROUP], e % GROUP) for e in range(E - GROUP)]
+        w_place = w_place + [(w_bf_late, 0), (w_bf_late, 1), (w_bf[2], 0), (w_bf[2], 1), (w_bf_shared, 0)]
+        w_raw = {}
+
+        def load_w(e):
+            w_raw[e] = wraw.tile([P, PACK, N], F32, name="w_raw")
+            nc.sync.dma_start(out=w_raw[e][:], in_=w[e].rearrange("(p j) n -> p j n", j=PACK))
+
+        for u in range(2):
+            nc.gpsimd.memset(pairs[:, 2 * (u * WIN + T) : 2 * (u + 1) * WIN], 0.0)
+        nc.gpsimd.memset(gate_rows[:], 0.0)
+        make_identity(nc, ident[:])
+
+        nc.sync.dma_start(out=x_raw[0][:], in_=x_rows[:, 0:2, :])
+        nc.sync.dma_start(offs_t[:], offs)
+        load_w(0)
+        nc.sync.dma_start(out=x_raw[1][:], in_=x_rows[:, 2:4, :])
+        load_w(1)
+        nc.sync.dma_start(out=bias[:, :, 0 : E + 1], in_=b.rearrange("(h p) e -> p h e", p=P))
+
+        def cast_x(copy, u):
+            dst = pairs[:, 2 * u * WIN : 2 * (u * WIN + T)].rearrange("p (t j) -> p t j", j=2)
+            copy(out=dst, in_=x_raw[u][:].rearrange("p j t -> p t j"))
+
+        words = pairs[:].bitcast(U32)
+        picked_tiles = [keep.tile([P, 2 * GS], U32, name=f"picked{i}") for i in range(2)]
+        picked = [picked_tiles[min(g, 1)] for g in range(GROUPS)]
+        woven0 = keep.tile([P, GS * PACK], BF16, name="woven0", align_bytes=64)
+        woven3 = keep.tile([P, GS * PACK], BF16, name="woven3", align_bytes=64)
+        woven = [woven0[:], w_bf[0][:, 0 : GS * PACK], w_bf[1][:, 0 : GS * PACK], woven3[:]]
+        x_bf = w_bf[0][:, GS * PACK : 2 * GS * PACK]
+        s_codes = {}
+        s_scales = {}
+
+        def gather(g, u):
+            cols = slice(g * GS // 16, (g + 1) * GS // 16)
+            nc.vector.tensor_copy(
+                out=picked[g][:, u * GS : (u + 1) * GS],
+                in_=words[:, u * WIN : (u + 1) * WIN].indirect(offs_t[:, cols]),
+            )
+
+        def weave(g):
+            nc.vector.tensor_copy(
+                out=woven[g].bitcast(I32).rearrange("p (s u) -> p s u", u=2),
+                in_=picked[g][:].bitcast(I32).rearrange("p (u s) -> p s u", u=2),
+            )
+
+        def quant_slots(g):
+            s_codes[g] = keep.tile([P, GS], U32, name=f"s_codes{g}", align_bytes=64)
+            s_scales[g] = keep.tile([P, GS], U8, name=f"s_scales{g}", align_bytes=64)
+            nc.vector.quantize_mx(out=s_codes[g][:].bitcast(FP8X4), scales=s_scales[g][:], in_=woven[g])
+
+        w_codes = {}
+        w_scales = {}
+
+        def cast_w(copy, e):
+            dst, i = w_place[e]
+            copy(
+                out=dst[:, i * WCOLS : (i + 1) * WCOLS].rearrange("p (c i j) -> p c j i", i=4, j=PACK),
+                in_=w_raw[e][:].rearrange("p j (c i) -> p c j i", i=4),
+            )
+
+        def quant_w(first, count):
+            src, i = w_place[first]
+            codes = keep.tile([P, count * N], U32, name=f"w_codes{first}", align_bytes=64)
+            scales = keep.tile([P, count * N], U8, name=f"w_scales{first}", align_bytes=64)
+            nc.vector.quantize_mx(
+                out=codes[:].bitcast(FP8X4), scales=scales[:], in_=src[:, i * WCOLS : (i + count) * WCOLS]
+            )
+            for m in range(count):
+                w_codes[first + m] = codes[:, m * N : (m + 1) * N]
+                w_scales[first + m] = scales[:, m * N : (m + 1) * N]
+
+        def experts_half(g, h, pool, tag):
+            rows = slice(h * P, (h + 1) * P)
+            acc = pool.tile([P, GROUP, C], F32, name=tag)
+            for i in range(GROUP):
+                e = g * GROUP + i
+                cols = slice(i * C, (i + 1) * C)
+                nc.tensor.matmul_mx(
+                    out=acc[:, i, :],
+                    lhsT=w_codes[e][:, rows].bitcast(FP8X4),
+                    lhsT_scale=w_scales[e][:, rows],
+                    rhs=s_codes[g][:, cols].bitcast(FP8X4),
+                    rhs_scale=s_scales[g][:, cols],
+                    start=True,
+                    stop=True,
+                )
+            for i in range(GROUP):
+                e = g * GROUP + i
+                nc.scalar.activation(
+                    out=y[h][:, e * C : (e + 1) * C], in_=acc[:, i, :], func=IDENT, bias=bias[:, h, e : e + 1]
+                )
+
+        cast_x(nc.vector.tensor_copy, 0)
+        gather(0, 0)
+        gather(1, 0)
+        cast_w(nc.scalar.copy, 0)
+        cast_x(nc.scalar.copy, 1)
+        gather(0, 1)
+        weave(0)
+        gather(1, 1)
+        quant_slots(0)
+
+        x_codes = keep.tile([P, T], U32, name="x_codes", align_bytes=64)
+        x_scales = keep.tile([P, T], U8, name="x_scales", align_bytes=64)
+
+        for g in range(GROUPS - 1):
+            experts = range(g * GROUP, (g + 1) * GROUP)
+            for e in experts:
+                if e > 1:
+                    load_w(e)
+                if e > 0:
+                    cast_w(nc.scalar.copy, e)
+            quant_w(g * GROUP, GROUP)
+            for h in range(HALVES):
+                experts_half(g, h, psum_a, "bank_a")
+            if g < GROUPS - 2:
+                weave(g + 1)
+                if g == 0:
+                    nc.vector.tensor_copy(
+                        out=x_bf.bitcast(I32).rearrange("p (t u) -> p t u", u=2),
+                        in_=pairs[:].bitcast(I32).rearrange("p (u t) -> p t u", u=2)[:, 0:T, :],
+                    )
+                    quant_slots(g + 1)
+                    gather(g + 2, 0)
+                    nc.vector.quantize_mx(out=x_codes[:].bitcast(FP8X4), scales=x_scales[:], in_=x_bf)
+                    gather(g + 2, 1)
+                    nc.sync.dma_start(out=gate_rows[0:TOP, :], in_=gate[:, 0, :])
+                    turned = psum_b.tile([P, T // P, P], F32, name="bank_b")
+                    for c in range(T // P):
+                        nc.tensor.transpose(turned[:, c, :], gate_rows[:, c * P : (c + 1) * P], ident[:])
+                    nc.scalar.copy(out=gate_cols[:], in_=turned[:, :, 0:TOP])
+                else:
+                    gather(g + 2, 0)
+                    quant_slots(g + 1)
+                    gather(g + 2, 1)
+                    weave(g + 2)
+                    quant_slots(g + 2)
+
+        last = range(E - GROUP, E)
+        for e in last:
+            load_w(e)
+        for r, pos in enumerate((pos1, pos2, pos3, pos4)):
+            nc.sync.dma_start(pos_t[r][:], pos)
+        load_w(E)
+        nc.sync.dma_start(out=gate_last[:], in_=gate[TOP - 1, 0:P, :])
+        for e in last:
+            cast_w(nc.scalar.copy if e < E - 2 else nc.vector.tensor_copy, e)
+        quant_w(E - 4, 2)
+        quant_w(E - 2, 2)
+        experts_half(GROUPS - 1, 0, psum_a, "bank_a")
+
+        cast_w(nc.scalar.copy, E)
+        experts_half(GROUPS - 1, 1, psum_b, "bank_b")
+        quant_w(E, 1)
+        shared_t = keep.tile([P, T // P, N], F32, name="shared_t")
+        for half in range(2):
+            bank = psum_b.tile([P, 2, N], F32, name="bank_b")
+            for i in range(2):
+                toks = slice((2 * half + i) * P, (2 * half + i + 1) * P)
+                nc.tensor.matmul_mx(
+                    out=bank[:, i, :],
+                    lhsT=x_codes[:, toks].bitcast(FP8X4),
+                    lhsT_scale=x_scales[:, toks],
+                    rhs=w_codes[E].bitcast(FP8X4),
+                    rhs_scale=w_scales[E],
+                    start=True,
+                    stop=True,
+                )
+            nc.scalar.copy(out=shared_t[:, 2 * half : 2 * half + 2, :], in_=bank[:])
+
+        units = [(h, q) for h in range(HALVES) for q in range(T // UNIT)]
+        sums = {}
+        direct = {}
+
+        def fetch(h, q):
+            cols = slice(q * UNIT // 16, (q + 1) * UNIT // 16)
+            gated = []
+            for r in range(TURNED):
+                if (h, q, r) == (0, 0, TURNED - 1):
+                    got = w_bf_shared[:].bitcast(F32)[:, 0:UNIT]
+                else:
+                    got = keep.tile([P, UNIT], F32, name=f"got{h}{q}{r}")[:]
+                nc.vector.tensor_copy(out=got, in_=y[h][:].indirect(pos_t[r][:, cols]))
+                flipped = psum_b.tile([P, BLOCKS, P], F32, name="bank_b")
+                for i in range(BLOCKS):
+                    nc.tensor.transpose(flipped[:, i, :], got[:, i * P : (i + 1) * P], ident[:])
+                gated.append(keep.tile([P, BLOCKS, P], F32, name=f"gated{h}{q}{r}"))
+                for i in range(BLOCKS):
+                    c = q * BLOCKS + i
+                    nc.scalar.activation(
+                        out=gated[r][:, i, :], in_=flipped[:, i, :], func=IDENT, scale=gate_cols[:, c, r : r + 1]
+                    )
+            direct[h, q] = keep.tile([P, UNIT], F32, name=f"direct{h}{q}")
+            nc.vector.tensor_tensor(
+                out=direct[h, q][:],
+                in0=y[h][:].indirect(pos_t[TURNED][:, cols]),
+                in1=gate_last[:, q * UNIT : (q + 1) * UNIT],
+                op=MULT,
+            )
+            sums[h, q] = psum_a.tile([P, BLOCKS, P], F32, name="bank_a")
+            for i in range(BLOCKS):
+                terms = [gated[r][:, i, :] for r in range(TURNED)]
+                terms.insert(TURNED - 1, shared_t[:, q * BLOCKS + i, h * P : (h + 1) * P])
+                for m, term in enumerate(terms):
+                    nc.tensor.matmul(
+                        sums[h, q][:, i, :],
+                        term,
+                        ident[:],
+                        start=(m == 0),
+                        stop=(m == len(terms) - 1),
+                        is_transpose=True,
+                    )
+
+        def finish(h, q):
+            result = keep.tile([P, UNIT], F32, name=f"result{h}{q}")
+            nc.vector.scalar_tensor_tensor(
+                out=result[:],
+                in0=sums[h, q][:].rearrange("p i t -> p (i t)"),
+                scalar=bias[:, h, E : E + 1],
+                in1=direct[h, q][:],
+                op0=ADD,
+                op1=ADD,
+            )
+            nc.sync.dma_start(out=out[h * P : (h + 1) * P, q * UNIT : (q + 1) * UNIT], in_=result[:])
+
+        for unit in units:
+            fetch(*unit)
+        for unit in units:
+            finish(*unit)

@@ -28,33 +28,31 @@ WIN = 704
 WCOLS = N * PACK
 UNIT = 256
 BLOCKS = UNIT // P
-TURNED = TOP - 1
 
 
 def tile_moe_shr_lin_bias_kernel(tc, xT, w, b, gate, offs, pos1, pos2, pos3, pos4, out):
     nc = tc.nc
     with ExitStack() as ctx:
         keep = ctx.enter_context(tc.tile_pool(name="keep", bufs=1))
-        wraw = ctx.enter_context(tc.tile_pool(name="wraw", bufs=12))
-        psum_a = ctx.enter_context(tc.psum_pool(name="psum_a", bufs=4))
-        psum_b = ctx.enter_context(tc.psum_pool(name="psum_b", bufs=4))
+        wraw = ctx.enter_context(tc.tile_pool(name="wraw", bufs=E + 1))
+        psum = ctx.enter_context(tc.psum_pool(name="psum", bufs=1))
+
+        def bank(number, shape):
+            return psum.tile(shape, F32, name=f"bank{number}")
 
         x_rows = xT.rearrange("(p j) t -> p j t", j=PACK)
         x_raw = [keep.tile([P, 2, T], F32, name=f"x_raw{u}") for u in range(2)]
         offs_t = keep.tile([P, S // 16], U16, name="offs_t")
         pos_t = [keep.tile([P, T // 16], U16, name=f"pos_t{r}") for r in range(TOP)]
-        bias = keep.tile([P, HALVES, 32], F32, name="bias")
-        gate_rows = keep.tile([P, T], F32, name="gate_rows")
-        gate_last = keep.tile([P, T], F32, name="gate_last")
-        gate_cols = keep.tile([P, T // P, TOP], F32, name="gate_cols")
+        bias = [keep.tile([P, HALVES, 8], F32, name=f"bias{g}") for g in range(GROUPS)]
+        gate_t = [keep.tile([P, T], F32, name=f"gate_t{r}") for r in range(TOP)]
         ident = keep.tile([P, P], F32, name="ident")
         pairs = keep.tile([P, 2 * WIN * 2], BF16, name="pairs", align_bytes=64)
         y = [keep.tile([P, S], F32, name=f"y{h}") for h in range(HALVES)]
         w_bf = [keep.tile([P, GROUP * WCOLS], BF16, name=f"w_bf{g}", align_bytes=64) for g in range(GROUPS - 1)]
         w_bf_late = keep.tile([P, 2 * WCOLS], BF16, name="w_bf_late", align_bytes=64)
-        w_bf_shared = keep.tile([P, WCOLS], BF16, name="w_bf_shared", align_bytes=64)
         w_place = [(w_bf[e // GROUP], e % GROUP) for e in range(E - GROUP)]
-        w_place = w_place + [(w_bf_late, 0), (w_bf_late, 1), (w_bf[2], 0), (w_bf[2], 1), (w_bf_shared, 0)]
+        w_place = w_place + [(w_bf_late, 1), (w_bf[2], 0), (w_bf[2], 1), (w_bf[2], 2), (w_bf_late, 0)]
         w_raw = {}
 
         def load_w(e):
@@ -63,7 +61,6 @@ def tile_moe_shr_lin_bias_kernel(tc, xT, w, b, gate, offs, pos1, pos2, pos3, pos
 
         for u in range(2):
             nc.gpsimd.memset(pairs[:, 2 * (u * WIN + T) : 2 * (u + 1) * WIN], 0.0)
-        nc.gpsimd.memset(gate_rows[:], 0.0)
         make_identity(nc, ident[:])
 
         nc.sync.dma_start(out=x_raw[0][:], in_=x_rows[:, 0:2, :])
@@ -71,11 +68,15 @@ def tile_moe_shr_lin_bias_kernel(tc, xT, w, b, gate, offs, pos1, pos2, pos3, pos
         load_w(0)
         nc.sync.dma_start(out=x_raw[1][:], in_=x_rows[:, 2:4, :])
         load_w(1)
-        nc.sync.dma_start(out=bias[:, :, 0 : E + 1], in_=b.rearrange("(h p) e -> p h e", p=P))
+        b_rows = b.rearrange("(h p) e -> p h e", p=P)
+
+        def load_bias(g):
+            count = GROUP + 1 if g == GROUPS - 1 else GROUP
+            nc.sync.dma_start(out=bias[g][:, :, 0:count], in_=b_rows[:, :, g * GROUP : g * GROUP + count])
 
         def cast_x(copy, u):
-            dst = pairs[:, 2 * u * WIN : 2 * (u * WIN + T)].rearrange("p (t j) -> p t j", j=2)
-            copy(out=dst, in_=x_raw[u][:].rearrange("p j t -> p t j"))
+            dst = pairs[:, 2 * u * WIN : 2 * (u * WIN + T)].rearrange("p (c i j) -> p c j i", i=4, j=2)
+            copy(out=dst, in_=x_raw[u][:].rearrange("p j (c i) -> p c j i", i=4))
 
         words = pairs[:].bitcast(U32)
         picked_tiles = [keep.tile([P, 2 * GS], U32, name=f"picked{i}") for i in range(2)]
@@ -96,8 +97,8 @@ def tile_moe_shr_lin_bias_kernel(tc, xT, w, b, gate, offs, pos1, pos2, pos3, pos
 
         def weave(g):
             nc.vector.tensor_copy(
-                out=woven[g].bitcast(I32).rearrange("p (s u) -> p s u", u=2),
-                in_=picked[g][:].bitcast(I32).rearrange("p (u s) -> p s u", u=2),
+                out=woven[g].bitcast(I32).rearrange("p (c i u) -> p c u i", i=4, u=2),
+                in_=picked[g][:].bitcast(I32).rearrange("p (u c i) -> p c u i", u=2, i=4),
             )
 
         def quant_slots(g):
@@ -115,20 +116,21 @@ def tile_moe_shr_lin_bias_kernel(tc, xT, w, b, gate, offs, pos1, pos2, pos3, pos
                 in_=w_raw[e][:].rearrange("p j (c i) -> p c j i", i=4),
             )
 
-        def quant_w(first, count):
+        def quant_w(members):
+            first, count = members[0], len(members)
             src, i = w_place[first]
             codes = keep.tile([P, count * N], U32, name=f"w_codes{first}", align_bytes=64)
             scales = keep.tile([P, count * N], U8, name=f"w_scales{first}", align_bytes=64)
             nc.vector.quantize_mx(
                 out=codes[:].bitcast(FP8X4), scales=scales[:], in_=src[:, i * WCOLS : (i + count) * WCOLS]
             )
-            for m in range(count):
-                w_codes[first + m] = codes[:, m * N : (m + 1) * N]
-                w_scales[first + m] = scales[:, m * N : (m + 1) * N]
+            for m, e in enumerate(members):
+                w_codes[e] = codes[:, m * N : (m + 1) * N]
+                w_scales[e] = scales[:, m * N : (m + 1) * N]
 
-        def experts_half(g, h, pool, tag):
+        def experts_half(g, h, number):
             rows = slice(h * P, (h + 1) * P)
-            acc = pool.tile([P, GROUP, C], F32, name=tag)
+            acc = bank(number, [P, GROUP, C])
             for i in range(GROUP):
                 e = g * GROUP + i
                 cols = slice(i * C, (i + 1) * C)
@@ -144,7 +146,7 @@ def tile_moe_shr_lin_bias_kernel(tc, xT, w, b, gate, offs, pos1, pos2, pos3, pos
             for i in range(GROUP):
                 e = g * GROUP + i
                 nc.scalar.activation(
-                    out=y[h][:, e * C : (e + 1) * C], in_=acc[:, i, :], func=IDENT, bias=bias[:, h, e : e + 1]
+                    out=y[h][:, e * C : (e + 1) * C], in_=acc[:, i, :], func=IDENT, bias=bias[g][:, h, i : i + 1]
                 )
 
         cast_x(nc.vector.tensor_copy, 0)
@@ -160,127 +162,122 @@ def tile_moe_shr_lin_bias_kernel(tc, xT, w, b, gate, offs, pos1, pos2, pos3, pos
         x_codes = keep.tile([P, T], U32, name="x_codes", align_bytes=64)
         x_scales = keep.tile([P, T], U8, name="x_scales", align_bytes=64)
 
-        for g in range(GROUPS - 1):
-            experts = range(g * GROUP, (g + 1) * GROUP)
-            for e in experts:
-                if e > 1:
-                    load_w(e)
-                if e > 0:
-                    cast_w(nc.scalar.copy, e)
-            quant_w(g * GROUP, GROUP)
-            for h in range(HALVES):
-                experts_half(g, h, psum_a, "bank_a")
-            if g < GROUPS - 2:
-                weave(g + 1)
-                if g == 0:
-                    nc.vector.tensor_copy(
-                        out=x_bf.bitcast(I32).rearrange("p (t u) -> p t u", u=2),
-                        in_=pairs[:].bitcast(I32).rearrange("p (u t) -> p t u", u=2)[:, 0:T, :],
-                    )
-                    quant_slots(g + 1)
-                    gather(g + 2, 0)
-                    nc.vector.quantize_mx(out=x_codes[:].bitcast(FP8X4), scales=x_scales[:], in_=x_bf)
-                    gather(g + 2, 1)
-                    nc.sync.dma_start(out=gate_rows[0:TOP, :], in_=gate[:, 0, :])
-                    turned = psum_b.tile([P, T // P, P], F32, name="bank_b")
-                    for c in range(T // P):
-                        nc.tensor.transpose(turned[:, c, :], gate_rows[:, c * P : (c + 1) * P], ident[:])
-                    nc.scalar.copy(out=gate_cols[:], in_=turned[:, :, 0:TOP])
-                else:
-                    gather(g + 2, 0)
-                    quant_slots(g + 1)
-                    gather(g + 2, 1)
-                    weave(g + 2)
-                    quant_slots(g + 2)
-
-        last = range(E - GROUP, E)
-        for e in last:
+        def load_cast(e):
             load_w(e)
+            cast_w(nc.scalar.copy, e)
+
+        cast_w(nc.scalar.copy, 1)
+        for e in (2, 3):
+            load_cast(e)
+        quant_w(range(0, 4))
+        weave(1)
+        nc.vector.tensor_copy(
+            out=x_bf.bitcast(I32).rearrange("p (c i u) -> p c u i", i=4, u=2),
+            in_=pairs[:].bitcast(I32).rearrange("p (u c i) -> p c u i", u=2, i=4)[:, 0 : T // 4, :, :],
+        )
+        quant_slots(1)
+        gather(2, 0)
+        nc.vector.quantize_mx(out=x_codes[:].bitcast(FP8X4), scales=x_scales[:], in_=x_bf)
+        gather(2, 1)
+        for e in (4, 5):
+            load_cast(e)
+        load_bias(0)
+        for h in range(HALVES):
+            experts_half(0, h, h)
+        for e in (6, 7):
+            load_cast(e)
+        quant_w(range(4, 8))
+        weave(2)
+        gather(3, 0)
+        quant_slots(2)
+        gather(3, 1)
+        weave(3)
+        quant_slots(3)
+        for e in (8, 9):
+            load_cast(e)
+        load_bias(1)
+        for h in range(HALVES):
+            experts_half(1, h, 2 + h)
+        for e in (10, 11):
+            load_cast(e)
+        quant_w(range(8, 12))
+        for e in (E, 12):
+            load_cast(e)
+        load_bias(2)
+        load_bias(3)
+        for h in range(HALVES):
+            experts_half(2, h, h)
+        for e in (13, 14, 15):
+            load_w(e)
+            cast_w(nc.vector.tensor_copy, e)
+            if e == 13:
+                quant_w((E, 12))
         for r, pos in enumerate((pos1, pos2, pos3, pos4)):
             nc.sync.dma_start(pos_t[r][:], pos)
-        load_w(E)
-        nc.sync.dma_start(out=gate_last[:], in_=gate[TOP - 1, 0:P, :])
-        for e in last:
-            cast_w(nc.scalar.copy if e < E - 2 else nc.vector.tensor_copy, e)
-        quant_w(E - 4, 2)
-        quant_w(E - 2, 2)
-        experts_half(GROUPS - 1, 0, psum_a, "bank_a")
+        for r in range(TOP):
+            nc.sync.dma_start(out=gate_t[r][:], in_=gate[r, 0:P, :])
+        quant_w((13, 14))
+        quant_w((15,))
+        for h in range(HALVES):
+            experts_half(GROUPS - 1, h, 4 + h)
 
-        cast_w(nc.scalar.copy, E)
-        experts_half(GROUPS - 1, 1, psum_b, "bank_b")
-        quant_w(E, 1)
-        shared_t = keep.tile([P, T // P, N], F32, name="shared_t")
-        for half in range(2):
-            bank = psum_b.tile([P, 2, N], F32, name="bank_b")
-            for i in range(2):
-                toks = slice((2 * half + i) * P, (2 * half + i + 1) * P)
-                nc.tensor.matmul_mx(
-                    out=bank[:, i, :],
-                    lhsT=x_codes[:, toks].bitcast(FP8X4),
-                    lhsT_scale=x_scales[:, toks],
-                    rhs=w_codes[E].bitcast(FP8X4),
-                    rhs_scale=w_scales[E],
-                    start=True,
-                    stop=True,
-                )
-            nc.scalar.copy(out=shared_t[:, 2 * half : 2 * half + 2, :], in_=bank[:])
+        shared = []
+        for h in range(HALVES):
+            rows = slice(h * P, (h + 1) * P)
+            shared_acc = bank(4 + h, [P, T])
+            nc.tensor.matmul_mx(
+                out=shared_acc[:],
+                lhsT=w_codes[E][:, rows].bitcast(FP8X4),
+                lhsT_scale=w_scales[E][:, rows],
+                rhs=x_codes[:].bitcast(FP8X4),
+                rhs_scale=x_scales[:],
+                start=True,
+                stop=True,
+            )
+            shared.append(keep.tile([P, T], F32, name=f"shared{h}"))
+            nc.scalar.activation(
+                out=shared[h][:], in_=shared_acc[:], func=IDENT, bias=bias[GROUPS - 1][:, h, GROUP : GROUP + 1]
+            )
 
         units = [(h, q) for h in range(HALVES) for q in range(T // UNIT)]
-        sums = {}
-        direct = {}
 
-        def fetch(h, q):
-            cols = slice(q * UNIT // 16, (q + 1) * UNIT // 16)
-            gated = []
-            for r in range(TURNED):
-                if (h, q, r) == (0, 0, TURNED - 1):
-                    got = w_bf_shared[:].bitcast(F32)[:, 0:UNIT]
-                else:
-                    got = keep.tile([P, UNIT], F32, name=f"got{h}{q}{r}")[:]
-                nc.vector.tensor_copy(out=got, in_=y[h][:].indirect(pos_t[r][:, cols]))
-                flipped = psum_b.tile([P, BLOCKS, P], F32, name="bank_b")
-                for i in range(BLOCKS):
-                    nc.tensor.transpose(flipped[:, i, :], got[:, i * P : (i + 1) * P], ident[:])
-                gated.append(keep.tile([P, BLOCKS, P], F32, name=f"gated{h}{q}{r}"))
-                for i in range(BLOCKS):
-                    c = q * BLOCKS + i
-                    nc.scalar.activation(
-                        out=gated[r][:, i, :], in_=flipped[:, i, :], func=IDENT, scale=gate_cols[:, c, r : r + 1]
-                    )
-            direct[h, q] = keep.tile([P, UNIT], F32, name=f"direct{h}{q}")
+        def gated_gather(h, q, r):
+            term = keep.tile([P, UNIT], F32, name=f"term{h}{q}{r}")
             nc.vector.tensor_tensor(
-                out=direct[h, q][:],
-                in0=y[h][:].indirect(pos_t[TURNED][:, cols]),
-                in1=gate_last[:, q * UNIT : (q + 1) * UNIT],
+                out=term[:],
+                in0=y[h][:].indirect(pos_t[r][:, q * UNIT // 16 : (q + 1) * UNIT // 16]),
+                in1=gate_t[r][:, q * UNIT : (q + 1) * UNIT],
                 op=MULT,
             )
-            sums[h, q] = psum_a.tile([P, BLOCKS, P], F32, name="bank_a")
-            for i in range(BLOCKS):
-                terms = [gated[r][:, i, :] for r in range(TURNED)]
-                terms.insert(TURNED - 1, shared_t[:, q * BLOCKS + i, h * P : (h + 1) * P])
-                for m, term in enumerate(terms):
-                    nc.tensor.matmul(
-                        sums[h, q][:, i, :],
-                        term,
-                        ident[:],
-                        start=(m == 0),
-                        stop=(m == len(terms) - 1),
-                        is_transpose=True,
-                    )
+            return term[:]
 
-        def finish(h, q):
-            result = keep.tile([P, UNIT], F32, name=f"result{h}{q}")
-            nc.vector.scalar_tensor_tensor(
-                out=result[:],
-                in0=sums[h, q][:].rearrange("p i t -> p (i t)"),
-                scalar=bias[:, h, E : E + 1],
-                in1=direct[h, q][:],
-                op0=ADD,
-                op1=ADD,
-            )
-            nc.sync.dma_start(out=out[h * P : (h + 1) * P, q * UNIT : (q + 1) * UNIT], in_=result[:])
-
-        for unit in units:
-            fetch(*unit)
-        for unit in units:
-            finish(*unit)
+        for n, (h, q) in enumerate(units):
+            toks = slice(q * UNIT, (q + 1) * UNIT)
+            result = keep.tile([P, UNIT], F32, name=f"result{n}")
+            if n + 1 < len(units):
+                terms = [shared[h][:, toks]] + [gated_gather(h, q, r) for r in range(TOP)]
+                turned_sum = bank(n, [P, BLOCKS, P])
+                for i in range(BLOCKS):
+                    for m, term in enumerate(terms):
+                        nc.tensor.matmul(
+                            turned_sum[:, i, :],
+                            term[:, i * P : (i + 1) * P],
+                            ident[:],
+                            start=(m == 0),
+                            stop=(m == TOP),
+                            is_transpose=True,
+                        )
+                turned = keep.tile([P, BLOCKS, P], F32, name=f"turned{n}")
+                nc.scalar.copy(out=turned[:], in_=turned_sum[:])
+                upright = bank((3, 6, 7)[n], [P, BLOCKS, P])
+                for i in range(BLOCKS):
+                    nc.tensor.transpose(upright[:, i, :], turned[:, i, :], ident[:])
+                nc.scalar.copy(out=result[:], in_=upright[:].rearrange("p i t -> p (i t)"))
+            else:
+                terms = [gated_gather(h, q, 0), gated_gather(h, q, 1)]
+                nc.vector.tensor_tensor(out=result[:], in0=terms[0], in1=shared[h][:, toks], op=ADD)
+                for r in range(2, TOP):
+                    terms.append(gated_gather(h, q, r))
+                    nc.vector.tensor_tensor(out=result[:], in0=result[:], in1=terms[r - 1], op=ADD)
+                nc.vector.tensor_tensor(out=result[:], in0=result[:], in1=terms[TOP - 1], op=ADD)
+            nc.sync.dma_start(out=out[h * P : (h + 1) * P, toks], in_=result[:])

@@ -20,12 +20,15 @@ IDENT = mybir.ActivationFunctionType.Identity
 
 P = 128
 PACK = 4
+LINE = 4
 HALVES = N // P
 GROUP = 4
 GROUPS = E // GROUP
+LAST = GROUPS - 1
 GS = GROUP * C
 WIN = 704
 WCOLS = N * PACK
+HCOLS = P * PACK
 UNIT = 256
 BLOCKS = UNIT // P
 
@@ -34,229 +37,242 @@ def tile_moe_shr_lin_bias_kernel(tc, xT, w, b, gate, offs, pos1, pos2, pos3, pos
     nc = tc.nc
     with ExitStack() as ctx:
         keep = ctx.enter_context(tc.tile_pool(name="keep", bufs=1))
-        wraw = ctx.enter_context(tc.tile_pool(name="wraw", bufs=E + 1))
         psum = ctx.enter_context(tc.psum_pool(name="psum", bufs=1))
 
         def bank(number, shape):
             return psum.tile(shape, F32, name=f"bank{number}")
 
-        x_rows = xT.rearrange("(p j) t -> p j t", j=PACK)
-        x_raw = [keep.tile([P, 2, T], F32, name=f"x_raw{u}") for u in range(2)]
         offs_t = keep.tile([P, S // 16], U16, name="offs_t")
         pos_t = [keep.tile([P, T // 16], U16, name=f"pos_t{r}") for r in range(TOP)]
-        bias = [keep.tile([P, HALVES, 8], F32, name=f"bias{g}") for g in range(GROUPS)]
-        gate_t = [keep.tile([P, T], F32, name=f"gate_t{r}") for r in range(TOP)]
+        x_raw = [keep.tile([P, 2, T], F32, name=f"x_raw{u}") for u in range(2)]
+        gate_t = [keep.tile([P, TOP, UNIT], F32, name=f"gate_t{q}") for q in range(T // UNIT)]
         ident = keep.tile([P, P], F32, name="ident")
         pairs = keep.tile([P, 2 * WIN * 2], BF16, name="pairs", align_bytes=64)
         y = [keep.tile([P, S], F32, name=f"y{h}") for h in range(HALVES)]
-        w_bf = [keep.tile([P, GROUP * WCOLS], BF16, name=f"w_bf{g}", align_bytes=64) for g in range(GROUPS - 1)]
-        w_bf_late = keep.tile([P, 2 * WCOLS], BF16, name="w_bf_late", align_bytes=64)
-        w_place = [(w_bf[e // GROUP], e % GROUP) for e in range(E - GROUP)]
-        w_place = w_place + [(w_bf_late, 1), (w_bf[2], 0), (w_bf[2], 1), (w_bf[2], 2), (w_bf_late, 0)]
+
+        early = keep.tile([P, 2 * GROUP * WCOLS], BF16, name="early", align_bytes=64)
+        third = keep.tile([P, GROUP * WCOLS], BF16, name="third", align_bytes=64)
+        late = [keep.tile([P, GROUP * HCOLS], BF16, name=f"late{h}", align_bytes=64) for h in range(HALVES)]
+        shared_bf = keep.tile([P, WCOLS], BF16, name="shared_bf", align_bytes=64)
+        woven0 = keep.tile([P, GS * PACK], BF16, name="woven0", align_bytes=64)
+        picked_tiles = [keep.tile([P, 2 * GS], U32, name=f"picked{i}") for i in range(2)]
+        group_bf = [early[:, 0 : 4 * WCOLS], early[:, 4 * WCOLS : 8 * WCOLS], third[:]]
+        woven = [woven0[:], early[:, 0 : 2 * WCOLS], early[:, 6 * WCOLS : 8 * WCOLS], late[0][:]]
+        picked = [
+            picked_tiles[0][:],
+            picked_tiles[1][:],
+            picked_tiles[1][:],
+            early[:, 3 * WCOLS : 5 * WCOLS].bitcast(U32),
+        ]
+        x_bf = late[0][:]
+
+        b_rows = b.rearrange("(h p) e -> p h e", p=P)
+        bias_early = [keep.tile([P, HALVES, 8], F32, name=f"bias{g}") for g in range(2)]
+        bias_third = keep.tile([P, 8], F32, name="bias_third")
+        bias_last = late[1][:].bitcast(F32).rearrange("p (i m) -> p i m", i=GROUP)
+        bias_rest = keep.tile([P, 16], F32, name="bias_rest")
+        bias_shared = keep.tile([P, 8], F32, name="bias_shared")
+
+        def bias_of(e, h):
+            g, i = divmod(e, GROUP)
+            if g < 2:
+                return bias_early[g][:, h, i : i + 1]
+            if h == 1:
+                return bias_rest[:, e - 2 * GROUP : e - 2 * GROUP + 1]
+            if e == E:
+                return bias_shared[:, 0:1]
+            if g == 2:
+                return bias_third[:, i : i + 1]
+            return bias_last[:, i, 0:1]
+
         w_raw = {}
 
-        def load_w(e):
-            w_raw[e] = wraw.tile([P, PACK, N], F32, name="w_raw")
-            nc.sync.dma_start(out=w_raw[e][:], in_=w[e].rearrange("(p j) n -> p j n", j=PACK))
+        def load_w(e, h=None):
+            cols = slice(0, N) if h is None else slice(h * P, (h + 1) * P)
+            w_raw[e, h] = keep.tile([P, PACK, cols.stop - cols.start], F32, name=f"w_raw{e}_{h}")
+            nc.sync.dma_start(out=w_raw[e, h][:], in_=w[e].rearrange("(p j) n -> p j n", j=PACK)[:, :, cols])
+
+        def load_gate(q):
+            nc.sync.dma_start(
+                out=gate_t[q][:], in_=gate[:, 0:P, q * UNIT : (q + 1) * UNIT].rearrange("r p t -> p r t")
+            )
+
+        def interleave(copy, dst, src, rows):
+            copy(
+                out=dst.rearrange("p (c i j) -> p c j i", i=LINE, j=rows),
+                in_=src.rearrange("p j (c i) -> p c j i", i=LINE),
+            )
+
+        def quantise(src, name):
+            width = src.shape[1] // PACK
+            codes = keep.tile([P, width], U32, name=f"codes_{name}", align_bytes=64)
+            scales = keep.tile([P, width], U8, name=f"scales_{name}", align_bytes=64)
+            nc.vector.quantize_mx(out=codes[:].bitcast(FP8X4), scales=scales[:], in_=src)
+            return codes, scales
+
+        def multiply(dst, stationary, s_cols, moving, m_cols):
+            nc.tensor.matmul_mx(
+                out=dst,
+                lhsT=stationary[0][:, s_cols].bitcast(FP8X4),
+                lhsT_scale=stationary[1][:, s_cols],
+                rhs=moving[0][:, m_cols].bitcast(FP8X4),
+                rhs_scale=moving[1][:, m_cols],
+                start=True,
+                stop=True,
+            )
+
+        def cast_x(copy, u):
+            interleave(copy, pairs[:, 2 * u * WIN : 2 * (u * WIN + T)], x_raw[u][:], 2)
+
+        def gather(g, u):
+            nc.vector.tensor_copy(
+                out=picked[g][:, u * GS : (u + 1) * GS],
+                in_=pairs[:].bitcast(U32)[:, u * WIN : (u + 1) * WIN].indirect(
+                    offs_t[:, g * GS // 16 : (g + 1) * GS // 16]
+                ),
+            )
+
+        def weave(g):
+            src = picked[g].bitcast(I32).rearrange("p (u s) -> p u s", u=2)
+            interleave(nc.vector.tensor_copy, woven[g].bitcast(I32), src, 2)
+
+        slots_q = {}
+
+        def quantise_slots(g):
+            slots_q[g] = quantise(woven[g], f"slots{g}")
+
+        def load_cast(e):
+            g, i = divmod(e, GROUP)
+            if (e, None) not in w_raw:
+                load_w(e)
+            interleave(nc.scalar.copy, group_bf[g][:, i * WCOLS : (i + 1) * WCOLS], w_raw[e, None][:], PACK)
+
+        def cast_half(copy, e, h):
+            i = e % GROUP
+            interleave(copy, late[h][:, i * HCOLS : (i + 1) * HCOLS], w_raw[e, h][:], PACK)
+
+        def products(g, h, weights_q, number):
+            acc = bank(number, [P, GROUP, C])
+            for i in range(GROUP):
+                first = i * P if g == LAST else i * N + h * P
+                multiply(acc[:, i, :], weights_q, slice(first, first + P), slots_q[g], slice(i * C, (i + 1) * C))
+            return acc
+
+        def add_bias(g, h, acc):
+            for i in range(GROUP):
+                e = g * GROUP + i
+                nc.scalar.activation(out=y[h][:, e * C : (e + 1) * C], in_=acc[:, i, :], func=IDENT, bias=bias_of(e, h))
 
         for u in range(2):
             nc.gpsimd.memset(pairs[:, 2 * (u * WIN + T) : 2 * (u + 1) * WIN], 0.0)
         make_identity(nc, ident[:])
 
+        x_rows = xT.rearrange("(p j) t -> p j t", j=PACK)
         nc.sync.dma_start(out=x_raw[0][:], in_=x_rows[:, 0:2, :])
         nc.sync.dma_start(offs_t[:], offs)
         load_w(0)
         nc.sync.dma_start(out=x_raw[1][:], in_=x_rows[:, 2:4, :])
-        load_w(1)
-        b_rows = b.rearrange("(h p) e -> p h e", p=P)
-
-        def load_bias(g):
-            count = GROUP + 1 if g == GROUPS - 1 else GROUP
-            nc.sync.dma_start(out=bias[g][:, :, 0:count], in_=b_rows[:, :, g * GROUP : g * GROUP + count])
-
-        def cast_x(copy, u):
-            dst = pairs[:, 2 * u * WIN : 2 * (u * WIN + T)].rearrange("p (c i j) -> p c j i", i=4, j=2)
-            copy(out=dst, in_=x_raw[u][:].rearrange("p j (c i) -> p c j i", i=4))
-
-        words = pairs[:].bitcast(U32)
-        picked_tiles = [keep.tile([P, 2 * GS], U32, name=f"picked{i}") for i in range(2)]
-        picked = [picked_tiles[min(g, 1)] for g in range(GROUPS)]
-        woven0 = keep.tile([P, GS * PACK], BF16, name="woven0", align_bytes=64)
-        woven3 = keep.tile([P, GS * PACK], BF16, name="woven3", align_bytes=64)
-        woven = [woven0[:], w_bf[0][:, 0 : GS * PACK], w_bf[1][:, 0 : GS * PACK], woven3[:]]
-        x_bf = w_bf[0][:, GS * PACK : 2 * GS * PACK]
-        s_codes = {}
-        s_scales = {}
-
-        def gather(g, u):
-            cols = slice(g * GS // 16, (g + 1) * GS // 16)
-            nc.vector.tensor_copy(
-                out=picked[g][:, u * GS : (u + 1) * GS],
-                in_=words[:, u * WIN : (u + 1) * WIN].indirect(offs_t[:, cols]),
-            )
-
-        def weave(g):
-            nc.vector.tensor_copy(
-                out=woven[g].bitcast(I32).rearrange("p (c i u) -> p c u i", i=4, u=2),
-                in_=picked[g][:].bitcast(I32).rearrange("p (u c i) -> p c u i", u=2, i=4),
-            )
-
-        def quant_slots(g):
-            s_codes[g] = keep.tile([P, GS], U32, name=f"s_codes{g}", align_bytes=64)
-            s_scales[g] = keep.tile([P, GS], U8, name=f"s_scales{g}", align_bytes=64)
-            nc.vector.quantize_mx(out=s_codes[g][:].bitcast(FP8X4), scales=s_scales[g][:], in_=woven[g])
-
-        w_codes = {}
-        w_scales = {}
-
-        def cast_w(copy, e):
-            dst, i = w_place[e]
-            copy(
-                out=dst[:, i * WCOLS : (i + 1) * WCOLS].rearrange("p (c i j) -> p c j i", i=4, j=PACK),
-                in_=w_raw[e][:].rearrange("p j (c i) -> p c j i", i=4),
-            )
-
-        def quant_w(members):
-            first, count = members[0], len(members)
-            src, i = w_place[first]
-            codes = keep.tile([P, count * N], U32, name=f"w_codes{first}", align_bytes=64)
-            scales = keep.tile([P, count * N], U8, name=f"w_scales{first}", align_bytes=64)
-            nc.vector.quantize_mx(
-                out=codes[:].bitcast(FP8X4), scales=scales[:], in_=src[:, i * WCOLS : (i + count) * WCOLS]
-            )
-            for m, e in enumerate(members):
-                w_codes[e] = codes[:, m * N : (m + 1) * N]
-                w_scales[e] = scales[:, m * N : (m + 1) * N]
-
-        def experts_half(g, h, number):
-            rows = slice(h * P, (h + 1) * P)
-            acc = bank(number, [P, GROUP, C])
-            for i in range(GROUP):
-                e = g * GROUP + i
-                cols = slice(i * C, (i + 1) * C)
-                nc.tensor.matmul_mx(
-                    out=acc[:, i, :],
-                    lhsT=w_codes[e][:, rows].bitcast(FP8X4),
-                    lhsT_scale=w_scales[e][:, rows],
-                    rhs=s_codes[g][:, cols].bitcast(FP8X4),
-                    rhs_scale=s_scales[g][:, cols],
-                    start=True,
-                    stop=True,
-                )
-            for i in range(GROUP):
-                e = g * GROUP + i
-                nc.scalar.activation(
-                    out=y[h][:, e * C : (e + 1) * C], in_=acc[:, i, :], func=IDENT, bias=bias[g][:, h, i : i + 1]
-                )
 
         cast_x(nc.vector.tensor_copy, 0)
         gather(0, 0)
         gather(1, 0)
-        cast_w(nc.scalar.copy, 0)
+        load_cast(0)
         cast_x(nc.scalar.copy, 1)
         gather(0, 1)
         weave(0)
         gather(1, 1)
-        quant_slots(0)
-
-        x_codes = keep.tile([P, T], U32, name="x_codes", align_bytes=64)
-        x_scales = keep.tile([P, T], U8, name="x_scales", align_bytes=64)
-
-        def load_cast(e):
-            load_w(e)
-            cast_w(nc.scalar.copy, e)
-
-        cast_w(nc.scalar.copy, 1)
-        for e in (2, 3):
+        quantise_slots(0)
+        for e in (1, 2, 3):
             load_cast(e)
-        quant_w(range(0, 4))
+        weights_q = quantise(group_bf[0], "w0")
+
         weave(1)
-        nc.vector.tensor_copy(
-            out=x_bf.bitcast(I32).rearrange("p (c i u) -> p c u i", i=4, u=2),
-            in_=pairs[:].bitcast(I32).rearrange("p (u c i) -> p c u i", u=2, i=4)[:, 0 : T // 4, :, :],
-        )
-        quant_slots(1)
+        gather(3, 0)
+        quantise_slots(1)
         gather(2, 0)
-        nc.vector.quantize_mx(out=x_codes[:].bitcast(FP8X4), scales=x_scales[:], in_=x_bf)
         gather(2, 1)
         for e in (4, 5):
             load_cast(e)
-        load_bias(0)
+        nc.sync.dma_start(out=bias_early[0][:, :, 0:GROUP], in_=b_rows[:, :, 0:GROUP])
         for h in range(HALVES):
-            experts_half(0, h, h)
+            add_bias(0, h, products(0, h, weights_q, h))
         for e in (6, 7):
             load_cast(e)
-        quant_w(range(4, 8))
+        weights_q = quantise(group_bf[1], "w1")
+
         weave(2)
-        gather(3, 0)
-        quant_slots(2)
         gather(3, 1)
+        quantise_slots(2)
         weave(3)
-        quant_slots(3)
+        quantise_slots(3)
         for e in (8, 9):
             load_cast(e)
-        load_bias(1)
-        for h in range(HALVES):
-            experts_half(1, h, 2 + h)
-        for e in (10, 11):
-            load_cast(e)
-        quant_w(range(8, 12))
-        for e in (E, 12):
-            load_cast(e)
-        load_bias(2)
-        load_bias(3)
-        for h in range(HALVES):
-            experts_half(2, h, h)
-        for e in (13, 14, 15):
-            load_w(e)
-            cast_w(nc.vector.tensor_copy, e)
-            if e == 13:
-                quant_w((E, 12))
+        nc.sync.dma_start(out=bias_early[1][:, :, 0:GROUP], in_=b_rows[:, :, GROUP : 2 * GROUP])
         for r, pos in enumerate((pos1, pos2, pos3, pos4)):
             nc.sync.dma_start(pos_t[r][:], pos)
-        for r in range(TOP):
-            nc.sync.dma_start(out=gate_t[r][:], in_=gate[r, 0:P, :])
-        quant_w((13, 14))
-        quant_w((15,))
         for h in range(HALVES):
-            experts_half(GROUPS - 1, h, 4 + h)
+            add_bias(1, h, products(1, h, weights_q, 2 + h))
+        for e in (10, 11):
+            load_cast(e)
+        weights_q = quantise(group_bf[2], "w2")
+
+        last = range(LAST * GROUP, E)
+        for e in last:
+            load_w(e, 0)
+            cast_half(nc.scalar.copy if e < E - 2 else nc.vector.tensor_copy, e, 0)
+            if e == E - 3:
+                nc.sync.dma_start(out=bias_third[:, 0:GROUP], in_=b_rows[:, 0, 2 * GROUP : 3 * GROUP])
+                nc.sync.dma_start(out=bias_last[:, :, 0:1], in_=b_rows[:, 0, 3 * GROUP : E].unsqueeze(2))
+        add_bias(2, 0, products(2, 0, weights_q, 0))
+        third_acc = products(2, 1, weights_q, 1)
+        add_bias(LAST, 0, products(LAST, 0, quantise(late[0][:], "w3_0"), 4))
+
+        src = pairs[:].bitcast(I32).rearrange("p (u t) -> p u t", u=2)[:, :, 0:T]
+        interleave(nc.vector.tensor_copy, x_bf.bitcast(I32), src, 2)
+        tokens_q = quantise(x_bf, "tokens")
+
+        load_gate(0)
+        load_w(E)
+        interleave(nc.scalar.copy, shared_bf[:], w_raw[E, None][:], PACK)
+        shared_q = quantise(shared_bf[:], "shared")
+        for e in last:
+            load_w(e, 1)
+            cast_half(nc.scalar.copy, e, 1)
+        nc.sync.dma_start(out=bias_rest[:, 0 : 2 * GROUP + 1], in_=b_rows[:, 1, 2 * GROUP : E + 1])
+        nc.sync.dma_start(out=bias_shared[:, 0:1], in_=b_rows[:, 0, E : E + 1])
+        load_gate(1)
+        add_bias(2, 1, third_acc)
+        add_bias(LAST, 1, products(LAST, 1, quantise(late[1][:], "w3_1"), 5))
 
         shared = []
         for h in range(HALVES):
-            rows = slice(h * P, (h + 1) * P)
-            shared_acc = bank(4 + h, [P, T])
-            nc.tensor.matmul_mx(
-                out=shared_acc[:],
-                lhsT=w_codes[E][:, rows].bitcast(FP8X4),
-                lhsT_scale=w_scales[E][:, rows],
-                rhs=x_codes[:].bitcast(FP8X4),
-                rhs_scale=x_scales[:],
-                start=True,
-                stop=True,
-            )
+            shared_acc = bank((1, 5)[h], [P, T])
+            multiply(shared_acc[:], shared_q, slice(h * P, (h + 1) * P), tokens_q, slice(0, T))
             shared.append(keep.tile([P, T], F32, name=f"shared{h}"))
-            nc.scalar.activation(
-                out=shared[h][:], in_=shared_acc[:], func=IDENT, bias=bias[GROUPS - 1][:, h, GROUP : GROUP + 1]
-            )
+            nc.scalar.activation(out=shared[h][:], in_=shared_acc[:], func=IDENT, bias=bias_of(E, h))
 
         units = [(h, q) for h in range(HALVES) for q in range(T // UNIT)]
 
-        def gated_gather(h, q, r):
-            term = keep.tile([P, UNIT], F32, name=f"term{h}{q}{r}")
+        def gated_gather(n, r):
+            h, q = units[n]
+            if n == 1 and r > 0:
+                term = late[1][:].bitcast(F32)[:, r * UNIT : (r + 1) * UNIT]
+            else:
+                term = keep.tile([P, UNIT], F32, name=f"term{n}{r}")[:]
             nc.vector.tensor_tensor(
-                out=term[:],
+                out=term,
                 in0=y[h][:].indirect(pos_t[r][:, q * UNIT // 16 : (q + 1) * UNIT // 16]),
-                in1=gate_t[r][:, q * UNIT : (q + 1) * UNIT],
+                in1=gate_t[q][:, r, :],
                 op=MULT,
             )
-            return term[:]
+            return term
 
         for n, (h, q) in enumerate(units):
             toks = slice(q * UNIT, (q + 1) * UNIT)
             result = keep.tile([P, UNIT], F32, name=f"result{n}")
             if n + 1 < len(units):
-                terms = [shared[h][:, toks]] + [gated_gather(h, q, r) for r in range(TOP)]
-                turned_sum = bank(n, [P, BLOCKS, P])
+                terms = [gated_gather(n, r) for r in range(TOP)] + [shared[h][:, toks]]
+                turned_sum = bank((0, 2, 3)[n], [P, BLOCKS, P])
                 for i in range(BLOCKS):
                     for m, term in enumerate(terms):
                         nc.tensor.matmul(
@@ -269,15 +285,15 @@ def tile_moe_shr_lin_bias_kernel(tc, xT, w, b, gate, offs, pos1, pos2, pos3, pos
                         )
                 turned = keep.tile([P, BLOCKS, P], F32, name=f"turned{n}")
                 nc.scalar.copy(out=turned[:], in_=turned_sum[:])
-                upright = bank((3, 6, 7)[n], [P, BLOCKS, P])
+                upright = bank((6, 7, 4)[n], [P, BLOCKS, P])
                 for i in range(BLOCKS):
                     nc.tensor.transpose(upright[:, i, :], turned[:, i, :], ident[:])
                 nc.scalar.copy(out=result[:], in_=upright[:].rearrange("p i t -> p (i t)"))
             else:
-                terms = [gated_gather(h, q, 0), gated_gather(h, q, 1)]
+                terms = [gated_gather(n, 0), gated_gather(n, 1)]
                 nc.vector.tensor_tensor(out=result[:], in0=terms[0], in1=shared[h][:, toks], op=ADD)
                 for r in range(2, TOP):
-                    terms.append(gated_gather(h, q, r))
+                    terms.append(gated_gather(n, r))
                     nc.vector.tensor_tensor(out=result[:], in0=result[:], in1=terms[r - 1], op=ADD)
                 nc.vector.tensor_tensor(out=result[:], in0=result[:], in1=terms[TOP - 1], op=ADD)
             nc.sync.dma_start(out=out[h * P : (h + 1) * P, toks], in_=result[:])

@@ -30,6 +30,7 @@ WIN = 704
 WCOLS = N * PACK
 HCOLS = P * PACK
 UNIT = 256
+SPLIT = 320
 BLOCKS = UNIT // P
 
 
@@ -50,26 +51,33 @@ def tile_moe_shr_lin_bias_kernel(tc, xT, w, b, gate, offs, pos1, pos2, pos3, pos
         pairs = keep.tile([P, 2 * WIN * 2], BF16, name="pairs", align_bytes=64)
         y = [keep.tile([P, S], F32, name=f"y{h}") for h in range(HALVES)]
 
-        early = keep.tile([P, 2 * GROUP * WCOLS], BF16, name="early", align_bytes=64)
-        third = keep.tile([P, GROUP * WCOLS], BF16, name="third", align_bytes=64)
-        late = [keep.tile([P, GROUP * HCOLS], BF16, name=f"late{h}", align_bytes=64) for h in range(HALVES)]
+        raw = keep.tile([P, (E + 1) * WCOLS], F32, name="raw", align_bytes=64)
+
+        def raw_cols(e, h=None):
+            if h is None:
+                return slice(e * WCOLS, (e + 1) * WCOLS)
+            first = LAST * GROUP * WCOLS + (h * GROUP + e % GROUP) * HCOLS
+            return slice(first, first + HCOLS)
+
+        def raw_span(first, count):
+            return raw[:, first * HCOLS : (first + count) * HCOLS]
+
+        group_bf = [keep.tile([P, GROUP * WCOLS], BF16, name=f"group_bf{g}", align_bytes=64)[:] for g in range(LAST)]
+        late = [raw_span(20, 2).bitcast(BF16), keep.tile([P, GROUP * HCOLS], BF16, name="late1", align_bytes=64)[:]]
         shared_bf = keep.tile([P, WCOLS], BF16, name="shared_bf", align_bytes=64)
-        woven0 = keep.tile([P, GS * PACK], BF16, name="woven0", align_bytes=64)
-        picked_tiles = [keep.tile([P, 2 * GS], U32, name=f"picked{i}") for i in range(2)]
-        group_bf = [early[:, 0 : 4 * WCOLS], early[:, 4 * WCOLS : 8 * WCOLS], third[:]]
-        woven = [woven0[:], early[:, 0 : 2 * WCOLS], early[:, 6 * WCOLS : 8 * WCOLS], late[0][:]]
+        woven = [keep.tile([P, GS * PACK], BF16, name=f"woven{g}", align_bytes=64)[:] for g in (0, 1, 3)]
+        woven.insert(2, raw_span(13, 2).bitcast(BF16))
         picked = [
-            picked_tiles[0][:],
-            picked_tiles[1][:],
-            picked_tiles[1][:],
-            early[:, 3 * WCOLS : 5 * WCOLS].bitcast(U32),
+            keep.tile([P, 2 * GS], U32, name=f"picked{g}")[:].rearrange("p (u s) -> p u s", u=2) for g in range(2)
         ]
-        x_bf = late[0][:]
+        picked.append(raw_span(5, 2).bitcast(U32).rearrange("p (u s) -> p u s", u=2))
+        picked.append(raw_span(7, 16).bitcast(U32).rearrange("p (u s) -> p u s", u=2)[:, :, 0:GS])
+        x_bf = late[0]
 
         b_rows = b.rearrange("(h p) e -> p h e", p=P)
         bias_early = [keep.tile([P, HALVES, 8], F32, name=f"bias{g}") for g in range(2)]
         bias_third = keep.tile([P, 8], F32, name="bias_third")
-        bias_last = late[1][:].bitcast(F32).rearrange("p (i m) -> p i m", i=GROUP)
+        bias_last = late[1].bitcast(F32).rearrange("p (i m) -> p i m", i=GROUP)
         bias_rest = keep.tile([P, 16], F32, name="bias_rest")
         bias_shared = keep.tile([P, 8], F32, name="bias_shared")
 
@@ -89,8 +97,8 @@ def tile_moe_shr_lin_bias_kernel(tc, xT, w, b, gate, offs, pos1, pos2, pos3, pos
 
         def load_w(e, h=None):
             cols = slice(0, N) if h is None else slice(h * P, (h + 1) * P)
-            w_raw[e, h] = keep.tile([P, PACK, cols.stop - cols.start], F32, name=f"w_raw{e}_{h}")
-            nc.sync.dma_start(out=w_raw[e, h][:], in_=w[e].rearrange("(p j) n -> p j n", j=PACK)[:, :, cols])
+            w_raw[e, h] = raw[:, raw_cols(e, h)].rearrange("p (j n) -> p j n", j=PACK)
+            nc.sync.dma_start(out=w_raw[e, h], in_=w[e].rearrange("(p j) n -> p j n", j=PACK)[:, :, cols])
 
         def load_gate(q):
             nc.sync.dma_start(
@@ -121,20 +129,19 @@ def tile_moe_shr_lin_bias_kernel(tc, xT, w, b, gate, offs, pos1, pos2, pos3, pos
                 stop=True,
             )
 
-        def cast_x(copy, u):
-            interleave(copy, pairs[:, 2 * u * WIN : 2 * (u * WIN + T)], x_raw[u][:], 2)
+        def cast_x(copy, u, first, stop):
+            interleave(copy, pairs[:, 2 * (u * WIN + first) : 2 * (u * WIN + stop)], x_raw[u][:, :, first:stop], 2)
 
         def gather(g, u):
             nc.vector.tensor_copy(
-                out=picked[g][:, u * GS : (u + 1) * GS],
+                out=picked[g][:, u, :],
                 in_=pairs[:].bitcast(U32)[:, u * WIN : (u + 1) * WIN].indirect(
                     offs_t[:, g * GS // 16 : (g + 1) * GS // 16]
                 ),
             )
 
         def weave(g):
-            src = picked[g].bitcast(I32).rearrange("p (u s) -> p u s", u=2)
-            interleave(nc.vector.tensor_copy, woven[g].bitcast(I32), src, 2)
+            interleave(nc.vector.tensor_copy, woven[g].bitcast(I32), picked[g].bitcast(I32), 2)
 
         slots_q = {}
 
@@ -145,11 +152,11 @@ def tile_moe_shr_lin_bias_kernel(tc, xT, w, b, gate, offs, pos1, pos2, pos3, pos
             g, i = divmod(e, GROUP)
             if (e, None) not in w_raw:
                 load_w(e)
-            interleave(nc.scalar.copy, group_bf[g][:, i * WCOLS : (i + 1) * WCOLS], w_raw[e, None][:], PACK)
+            interleave(nc.scalar.copy, group_bf[g][:, i * WCOLS : (i + 1) * WCOLS], w_raw[e, None], PACK)
 
         def cast_half(copy, e, h):
             i = e % GROUP
-            interleave(copy, late[h][:, i * HCOLS : (i + 1) * HCOLS], w_raw[e, h][:], PACK)
+            interleave(copy, late[h][:, i * HCOLS : (i + 1) * HCOLS], w_raw[e, h], PACK)
 
         def products(g, h, weights_q, number):
             acc = bank(number, [P, GROUP, C])
@@ -173,59 +180,57 @@ def tile_moe_shr_lin_bias_kernel(tc, xT, w, b, gate, offs, pos1, pos2, pos3, pos
         load_w(0)
         nc.sync.dma_start(out=x_raw[1][:], in_=x_rows[:, 2:4, :])
 
-        cast_x(nc.vector.tensor_copy, 0)
+        cast_x(nc.vector.tensor_copy, 0, 0, SPLIT)
+        cast_x(nc.scalar.copy, 0, SPLIT, T)
         gather(0, 0)
         gather(1, 0)
         load_cast(0)
-        cast_x(nc.scalar.copy, 1)
+        cast_x(nc.scalar.copy, 1, 0, T)
         gather(0, 1)
-        weave(0)
         gather(1, 1)
+        weave(0)
+        weave(1)
         quantise_slots(0)
+        quantise_slots(1)
         for e in (1, 2, 3):
             load_cast(e)
-        weights_q = quantise(group_bf[0], "w0")
+        first_q = quantise(group_bf[0], "w0")
 
-        weave(1)
-        gather(3, 0)
-        quantise_slots(1)
         gather(2, 0)
         gather(2, 1)
-        for e in (4, 5):
+        gather(3, 0)
+        for e in (4, 5, 6, 7):
             load_cast(e)
         nc.sync.dma_start(out=bias_early[0][:, :, 0:GROUP], in_=b_rows[:, :, 0:GROUP])
+        second_q = quantise(group_bf[1], "w1")
         for h in range(HALVES):
-            add_bias(0, h, products(0, h, weights_q, h))
-        for e in (6, 7):
-            load_cast(e)
-        weights_q = quantise(group_bf[1], "w1")
+            add_bias(0, h, products(0, h, first_q, h))
 
-        weave(2)
         gather(3, 1)
-        quantise_slots(2)
+        weave(2)
         weave(3)
+        quantise_slots(2)
         quantise_slots(3)
-        for e in (8, 9):
+        for e in (8, 9, 10, 11):
             load_cast(e)
+            if e == 9:
+                for r, pos in enumerate((pos1, pos2, pos3, pos4)):
+                    nc.sync.dma_start(pos_t[r][:], pos)
         nc.sync.dma_start(out=bias_early[1][:, :, 0:GROUP], in_=b_rows[:, :, GROUP : 2 * GROUP])
-        for r, pos in enumerate((pos1, pos2, pos3, pos4)):
-            nc.sync.dma_start(pos_t[r][:], pos)
-        for h in range(HALVES):
-            add_bias(1, h, products(1, h, weights_q, 2 + h))
-        for e in (10, 11):
-            load_cast(e)
         weights_q = quantise(group_bf[2], "w2")
+        for h in range(HALVES):
+            add_bias(1, h, products(1, h, second_q, 2 + h))
 
         last = range(LAST * GROUP, E)
         for e in last:
             load_w(e, 0)
-            cast_half(nc.scalar.copy if e < E - 2 else nc.vector.tensor_copy, e, 0)
+            cast_half(nc.scalar.copy if e == LAST * GROUP else nc.vector.tensor_copy, e, 0)
             if e == E - 3:
                 nc.sync.dma_start(out=bias_third[:, 0:GROUP], in_=b_rows[:, 0, 2 * GROUP : 3 * GROUP])
                 nc.sync.dma_start(out=bias_last[:, :, 0:1], in_=b_rows[:, 0, 3 * GROUP : E].unsqueeze(2))
         add_bias(2, 0, products(2, 0, weights_q, 0))
         third_acc = products(2, 1, weights_q, 1)
-        add_bias(LAST, 0, products(LAST, 0, quantise(late[0][:], "w3_0"), 4))
+        add_bias(LAST, 0, products(LAST, 0, quantise(late[0], "w3_0"), 4))
 
         src = pairs[:].bitcast(I32).rearrange("p (u t) -> p u t", u=2)[:, :, 0:T]
         interleave(nc.vector.tensor_copy, x_bf.bitcast(I32), src, 2)
@@ -233,7 +238,7 @@ def tile_moe_shr_lin_bias_kernel(tc, xT, w, b, gate, offs, pos1, pos2, pos3, pos
 
         load_gate(0)
         load_w(E)
-        interleave(nc.scalar.copy, shared_bf[:], w_raw[E, None][:], PACK)
+        interleave(nc.scalar.copy, shared_bf[:], w_raw[E, None], PACK)
         shared_q = quantise(shared_bf[:], "shared")
         for e in last:
             load_w(e, 1)
@@ -242,7 +247,7 @@ def tile_moe_shr_lin_bias_kernel(tc, xT, w, b, gate, offs, pos1, pos2, pos3, pos
         nc.sync.dma_start(out=bias_shared[:, 0:1], in_=b_rows[:, 0, E : E + 1])
         load_gate(1)
         add_bias(2, 1, third_acc)
-        add_bias(LAST, 1, products(LAST, 1, quantise(late[1][:], "w3_1"), 5))
+        add_bias(LAST, 1, products(LAST, 1, quantise(late[1], "w3_1"), 5))
 
         shared = []
         for h in range(HALVES):
@@ -256,7 +261,7 @@ def tile_moe_shr_lin_bias_kernel(tc, xT, w, b, gate, offs, pos1, pos2, pos3, pos
         def gated_gather(n, r):
             h, q = units[n]
             if n == 1 and r > 0:
-                term = late[1][:].bitcast(F32)[:, r * UNIT : (r + 1) * UNIT]
+                term = raw_span(30, 2)[:, r * UNIT : (r + 1) * UNIT]
             else:
                 term = keep.tile([P, UNIT], F32, name=f"term{n}{r}")[:]
             nc.vector.tensor_tensor(

from contextlib import ExitStack

import concourse.mybir as mybir
from concourse.masks import make_identity

K, T, E, C, N, TOP = 512, 512, 16, 128, 256, 4
S = E * C
FLOPS = 2 * K * N * (S + T)

F32 = mybir.dt.float32
BF16 = mybir.dt.bfloat16
I32 = mybir.dt.int32
U32 = mybir.dt.uint32
U16 = mybir.dt.uint16
U8 = mybir.dt.uint8
FP8X4 = mybir.dt.float8_e4m3fn_x4
ADD = mybir.AluOpType.add
MULT = mybir.AluOpType.mult
IDENT = mybir.ActivationFunctionType.Identity

P = 128
PACK = 4
LINE = 4
HALVES = N // P
GROUP = 4
GROUPS = E // GROUP
LAST = GROUPS - 1
GS = GROUP * C
WIN = 704
WCOLS = N * PACK
HCOLS = P * PACK
UNIT = 256
SPLIT = 320
BLOCKS = UNIT // P


def tile_moe_shr_lin_bias_kernel(tc, xT, w, b, gate, offs, pos1, pos2, pos3, pos4, out):
    nc = tc.nc
    with ExitStack() as ctx:
        keep = ctx.enter_context(tc.tile_pool(name="keep", bufs=1))
        psum = ctx.enter_context(tc.psum_pool(name="psum", bufs=1))

        def bank(number, shape):
            return psum.tile(shape, F32, name=f"bank{number}")

        offs_t = keep.tile([P, S // 16], U16, name="offs_t")
        pos_t = [keep.tile([P, T // 16], U16, name=f"pos_t{r}") for r in range(TOP)]
        x_raw = [keep.tile([P, 2, T], F32, name=f"x_raw{u}") for u in range(2)]
        gate_t = [keep.tile([P, TOP, UNIT], F32, name=f"gate_t{q}") for q in range(T // UNIT)]
        ident = keep.tile([P, P], F32, name="ident")
        pairs = keep.tile([P, 2 * WIN * 2], BF16, name="pairs", align_bytes=64)
        y = [keep.tile([P, S], F32, name=f"y{h}") for h in range(HALVES)]

        raw = keep.tile([P, (E + 1) * WCOLS], F32, name="raw", align_bytes=64)

        def raw_cols(e, h=None):
            if h is None:
                return slice(e * WCOLS, (e + 1) * WCOLS)
            first = LAST * GROUP * WCOLS + (h * GROUP + e % GROUP) * HCOLS
            return slice(first, first + HCOLS)

        def raw_span(first, count):
            return raw[:, first * HCOLS : (first + count) * HCOLS]

        group_bf = [keep.tile([P, GROUP * WCOLS], BF16, name=f"group_bf{g}", align_bytes=64)[:] for g in range(LAST)]
        late = [raw_span(20, 2).bitcast(BF16), keep.tile([P, GROUP * HCOLS], BF16, name="late1", align_bytes=64)[:]]
        shared_bf = keep.tile([P, WCOLS], BF16, name="shared_bf", align_bytes=64)
        woven = [keep.tile([P, GS * PACK], BF16, name=f"woven{g}", align_bytes=64)[:] for g in (0, 1, 3)]
        woven.insert(2, raw_span(13, 2).bitcast(BF16))
        picked = [
            keep.tile([P, 2 * GS], U32, name=f"picked{g}")[:].rearrange("p (u s) -> p u s", u=2) for g in range(2)
        ]
        picked.append(raw_span(5, 2).bitcast(U32).rearrange("p (u s) -> p u s", u=2))
        picked.append(raw_span(7, 16).bitcast(U32).rearrange("p (u s) -> p u s", u=2)[:, :, 0:GS])
        x_bf = late[0]

        b_rows = b.rearrange("(h p) e -> p h e", p=P)
        bias_early = [keep.tile([P, HALVES, 8], F32, name=f"bias{g}") for g in range(2)]
        bias_third = keep.tile([P, 8], F32, name="bias_third")
        bias_last = late[1].bitcast(F32).rearrange("p (i m) -> p i m", i=GROUP)
        bias_rest = keep.tile([P, 16], F32, name="bias_rest")
        bias_shared = keep.tile([P, 8], F32, name="bias_shared")

        def bias_of(e, h):
            g, i = divmod(e, GROUP)
            if g < 2:
                return bias_early[g][:, h, i : i + 1]
            if h == 1:
                return bias_rest[:, e - 2 * GROUP : e - 2 * GROUP + 1]
            if e == E:
                return bias_shared[:, 0:1]
            if g == 2:
                return bias_third[:, i : i + 1]
            return bias_last[:, i, 0:1]

        w_raw = {}

        def load_w(e, h=None):
            cols = slice(0, N) if h is None else slice(h * P, (h + 1) * P)
            w_raw[e, h] = raw[:, raw_cols(e, h)].rearrange("p (j n) -> p j n", j=PACK)
            nc.sync.dma_start(out=w_raw[e, h], in_=w[e].rearrange("(p j) n -> p j n", j=PACK)[:, :, cols])

        def load_gate(q):
            nc.sync.dma_start(
                out=gate_t[q][:], in_=gate[:, 0:P, q * UNIT : (q + 1) * UNIT].rearrange("r p t -> p r t")
            )

        def interleave(copy, dst, src, rows):
            copy(
                out=dst.rearrange("p (c i j) -> p c j i", i=LINE, j=rows),
                in_=src.rearrange("p j (c i) -> p c j i", i=LINE),
            )

        def quantise(src, name):
            width = src.shape[1] // PACK
            codes = keep.tile([P, width], U32, name=f"codes_{name}", align_bytes=64)
            scales = keep.tile([P, width], U8, name=f"scales_{name}", align_bytes=64)
            nc.vector.quantize_mx(out=codes[:].bitcast(FP8X4), scales=scales[:], in_=src)
            return codes, scales

        def multiply(dst, stationary, s_cols, moving, m_cols):
            nc.tensor.matmul_mx(
                out=dst,
                lhsT=stationary[0][:, s_cols].bitcast(FP8X4),
                lhsT_scale=stationary[1][:, s_cols],
                rhs=moving[0][:, m_cols].bitcast(FP8X4),
                rhs_scale=moving[1][:, m_cols],
                start=True,
                stop=True,
            )

        def cast_x(copy, u, first, stop):
            interleave(copy, pairs[:, 2 * (u * WIN + first) : 2 * (u * WIN + stop)], x_raw[u][:, :, first:stop], 2)

        def gather(g, u):
            nc.vector.tensor_copy(
                out=picked[g][:, u, :],
                in_=pairs[:].bitcast(U32)[:, u * WIN : (u + 1) * WIN].indirect(
                    offs_t[:, g * GS // 16 : (g + 1) * GS // 16]
                ),
            )

        def weave(g):
            interleave(nc.vector.tensor_copy, woven[g].bitcast(I32), picked[g].bitcast(I32), 2)

        slots_q = {}

        def quantise_slots(g):
            slots_q[g] = quantise(woven[g], f"slots{g}")

        def load_cast(e):
            g, i = divmod(e, GROUP)
            if (e, None) not in w_raw:
                load_w(e)
            interleave(nc.scalar.copy, group_bf[g][:, i * WCOLS : (i + 1) * WCOLS], w_raw[e, None], PACK)

        def cast_half(copy, e, h):
            i = e % GROUP
            interleave(copy, late[h][:, i * HCOLS : (i + 1) * HCOLS], w_raw[e, h], PACK)

        def products(g, h, weights_q, number):
            acc = bank(number, [P, GROUP, C])
            for i in range(GROUP):
                first = i * P if g == LAST else i * N + h * P
                multiply(acc[:, i, :], weights_q, slice(first, first + P), slots_q[g], slice(i * C, (i + 1) * C))
            return acc

        def add_bias(g, h, acc):
            for i in range(GROUP):
                e = g * GROUP + i
                nc.scalar.activation(out=y[h][:, e * C : (e + 1) * C], in_=acc[:, i, :], func=IDENT, bias=bias_of(e, h))

        for u in range(2):
            nc.gpsimd.memset(pairs[:, 2 * (u * WIN + T) : 2 * (u + 1) * WIN], 0.0)
        make_identity(nc, ident[:])

        x_rows = xT.rearrange("(p j) t -> p j t", j=PACK)
        nc.sync.dma_start(out=x_raw[0][:], in_=x_rows[:, 0:2, :])
        nc.sync.dma_start(offs_t[:], offs)
        load_w(0)
        nc.sync.dma_start(out=x_raw[1][:], in_=x_rows[:, 2:4, :])

        cast_x(nc.vector.tensor_copy, 0, 0, SPLIT)
        cast_x(nc.scalar.copy, 0, SPLIT, T)
        gather(0, 0)
        gather(1, 0)
        load_cast(0)
        cast_x(nc.scalar.copy, 1, 0, T)
        gather(0, 1)
        gather(1, 1)
        weave(0)
        weave(1)
        quantise_slots(0)
        quantise_slots(1)
        for e in (1, 2, 3):
            load_cast(e)
        first_q = quantise(group_bf[0], "w0")

        gather(2, 0)
        gather(2, 1)
        gather(3, 0)
        for e in (4, 5, 6, 7):
            load_cast(e)
        nc.sync.dma_start(out=bias_early[0][:, :, 0:GROUP], in_=b_rows[:, :, 0:GROUP])
        second_q = quantise(group_bf[1], "w1")
        for h in range(HALVES):
            add_bias(0, h, products(0, h, first_q, h))

        gather(3, 1)
        weave(2)
        weave(3)
        quantise_slots(2)
        quantise_slots(3)
        for e in (8, 9, 10, 11):
            load_cast(e)
            if e == 9:
                for r, pos in enumerate((pos1, pos2, pos3, pos4)):
                    nc.sync.dma_start(pos_t[r][:], pos)
        nc.sync.dma_start(out=bias_early[1][:, :, 0:GROUP], in_=b_rows[:, :, GROUP : 2 * GROUP])
        weights_q = quantise(group_bf[2], "w2")
        for h in range(HALVES):
            add_bias(1, h, products(1, h, second_q, 2 + h))

        last = range(LAST * GROUP, E)
        for e in last:
            load_w(e, 0)
            cast_half(nc.scalar.copy if e == LAST * GROUP else nc.vector.tensor_copy, e, 0)
            if e == E - 3:
                nc.sync.dma_start(out=bias_third[:, 0:GROUP], in_=b_rows[:, 0, 2 * GROUP : 3 * GROUP])
                nc.sync.dma_start(out=bias_last[:, :, 0:1], in_=b_rows[:, 0, 3 * GROUP : E].unsqueeze(2))
        add_bias(2, 0, products(2, 0, weights_q, 0))
        third_acc = products(2, 1, weights_q, 1)
        add_bias(LAST, 0, products(LAST, 0, quantise(late[0], "w3_0"), 4))

        src = pairs[:].bitcast(I32).rearrange("p (u t) -> p u t", u=2)[:, :, 0:T]
        interleave(nc.vector.tensor_copy, x_bf.bitcast(I32), src, 2)
        tokens_q = quantise(x_bf, "tokens")

        load_gate(0)
        load_w(E)
        interleave(nc.scalar.copy, shared_bf[:], w_raw[E, None], PACK)
        shared_q = quantise(shared_bf[:], "shared")
        for e in last:
            load_w(e, 1)
            cast_half(nc.scalar.copy, e, 1)
        nc.sync.dma_start(out=bias_rest[:, 0 : 2 * GROUP + 1], in_=b_rows[:, 1, 2 * GROUP : E + 1])
        nc.sync.dma_start(out=bias_shared[:, 0:1], in_=b_rows[:, 0, E : E + 1])
        load_gate(1)
        add_bias(2, 1, third_acc)
        add_bias(LAST, 1, products(LAST, 1, quantise(late[1], "w3_1"), 5))

        shared = []
        for h in range(HALVES):
            shared_acc = bank((1, 5)[h], [P, T])
            multiply(shared_acc[:], shared_q, slice(h * P, (h + 1) * P), tokens_q, slice(0, T))
            shared.append(keep.tile([P, T], F32, name=f"shared{h}"))
            nc.scalar.activation(out=shared[h][:], in_=shared_acc[:], func=IDENT, bias=bias_of(E, h))

        units = [(h, q) for h in range(HALVES) for q in range(T // UNIT)]

        def gated_gather(n, r):
            h, q = units[n]
            if n == 1 and r > 0:
                term = raw_span(30, 2)[:, r * UNIT : (r + 1) * UNIT]
            else:
                term = keep.tile([P, UNIT], F32, name=f"term{n}{r}")[:]
            nc.vector.tensor_tensor(
                out=term,
                in0=y[h][:].indirect(pos_t[r][:, q * UNIT // 16 : (q + 1) * UNIT // 16]),
                in1=gate_t[q][:, r, :],
                op=MULT,
            )
            return term

        for n, (h, q) in enumerate(units):
            toks = slice(q * UNIT, (q + 1) * UNIT)
            result = keep.tile([P, UNIT], F32, name=f"result{n}")
            if n + 1 < len(units):
                terms = [gated_gather(n, r) for r in range(TOP)] + [shared[h][:, toks]]
                turned_sum = bank((0, 2, 3)[n], [P, BLOCKS, P])
                for i in range(BLOCKS):
                    for m, term in enumerate(terms):
                        nc.tensor.matmul(
                            turned_sum[:, i, :],
                            term[:, i * P : (i + 1) * P],
                            ident[:],
                            start=(m == 0),
                            stop=(m == TOP),
                            is_transpose=True,
                        )
                turned = keep.tile([P, BLOCKS, P], F32, name=f"turned{n}")
                nc.scalar.copy(out=turned[:], in_=turned_sum[:])
                upright = bank((6, 7, 4)[n], [P, BLOCKS, P])
                for i in range(BLOCKS):
                    nc.tensor.transpose(upright[:, i, :], turned[:, i, :], ident[:])
                nc.scalar.copy(out=result[:], in_=upright[:].rearrange("p i t -> p (i t)"))
            else:
                terms = [gated_gather(n, 0), gated_gather(n, 1)]
                nc.vector.tensor_tensor(out=result[:], in0=terms[0], in1=shared[h][:, toks], op=ADD)
                for r in range(2, TOP):
                    terms.append(gated_gather(n, r))
                    nc.vector.tensor_tensor(out=result[:], in0=result[:], in1=terms[r - 1], op=ADD)
                nc.vector.tensor_tensor(out=result[:], in0=result[:], in1=terms[TOP - 1], op=ADD)
            nc.sync.dma_start(out=out[h * P : (h + 1) * P, toks], in_=result[:])
